import numpy as np
import ml_dtypes


def mxq(x, axis, fmt="e4m3"):
    dtype, down = {"e4m3": (ml_dtypes.float8_e4m3fn, 7), "e5m2": (ml_dtypes.float8_e5m2, 14)}[fmt]
    v = np.moveaxis(np.asarray(x, np.float32).astype(ml_dtypes.bfloat16).astype(np.float64), axis, -1)
    blocks = v.reshape(v.shape[:-1] + (-1, 32))
    amax = np.abs(blocks).max(-1, keepdims=True)
    byte = np.maximum(np.where(amax > 0, np.frexp(amax)[1] - 1 + 127, 0) - down, 1)
    scale = np.exp2(byte - 127.0)
    codes = (blocks / scale).astype(np.float32).astype(dtype).astype(np.float64)
    return np.moveaxis((codes * scale).reshape(v.shape), -1, axis)


WIDE = False


def mx_kscale(k):
    if not WIDE:
        return np.ones(k)
    levels = np.array([24, -24, 12, -12, 0])
    if k % 512:
        return np.exp2(np.random.permutation(np.resize(levels, k // 32))).repeat(32)
    a = np.empty((k // 512, 16))
    for p in range(k // 512):
        a[p, :8] = np.random.permutation(np.resize(levels, 8))
        for g in range(8):
            far = levels[np.abs(levels - a[p, g]) >= 10]
            a[p, g + 8] = far[np.random.randint(len(far))]
    return np.exp2(a.ravel()).repeat(32)


def f64(x):
    return np.asarray(x).astype(np.float64)


def striped8(idx):
    return np.concatenate([v.reshape(-1, 16).T for v in idx]).astype(np.uint16)


def unstriped8(offs):
    return np.stack([offs[16 * g:16 * g + 16].T.reshape(-1) for g in range(8)]).astype(np.int64)


E2M1 = np.array([0.0, 0.5, 1.0, 1.5, 2.0, 3.0, 4.0, 6.0, -0.0, -0.5, -1.0, -1.5, -2.0, -3.0, -4.0, -6.0])


def pack_weight(w, fmt):
    k, n = w.shape
    w = f64(np.asarray(w, np.float32).astype(ml_dtypes.bfloat16)).reshape(k // 32, 32, n)
    amax = np.abs(w).max(1)
    if fmt == "e4m3":
        byte = np.frexp(amax)[1] - 1 + 127 - 7
    else:
        mant, ex = np.frexp(amax / 6.0)
        byte = np.where(mant > 0.5, ex, ex - 1) + 127
    byte = np.clip(np.where(amax > 0, byte, 1), 1, 254)
    scaled = (w * np.exp2(127.0 - byte)[:, None, :]).reshape(k, n).astype(np.float32)
    by_word = np.ascontiguousarray(scaled.reshape(k // 512, 128, 4, n).transpose(0, 1, 3, 2))
    if fmt == "e4m3":
        words = by_word.astype(ml_dtypes.float8_e4m3fn).view(np.uint8)
    else:
        c = by_word.astype(ml_dtypes.float4_e2m1fn).view(np.uint8) & 0xF
        words = (c[..., 0::2] | (c[..., 1::2] << 4)).reshape(k // 512, 128, 2 * n)
    return np.ascontiguousarray(words), np.ascontiguousarray(byte.astype(np.uint8).reshape(k // 512, 16, n))


def unpack_weight(words, scales, fmt):
    g, _, n = scales.shape
    words = np.ascontiguousarray(words).reshape(g, 128, n, -1)
    if fmt == "e4m3":
        vals = words.view(ml_dtypes.float8_e4m3fn).astype(np.float64)
    else:
        nib = np.empty((g, 128, n, 4), np.uint8)
        nib[..., 0::2] = words & 0xF
        nib[..., 1::2] = words >> 4
        vals = E2M1[nib]
    vals = vals * np.repeat(np.exp2(scales.astype(np.float64) - 127.0), 8, axis=1)[..., None]
    return vals.transpose(0, 1, 3, 2).reshape(g * 512, n)


def gelu(f):
    return 0.5 * f * (1.0 + np.tanh(np.sqrt(2.0 / np.pi) * (f + 0.044715 * f**3)))


K, N, T, J = 512, 512, 2048, 512


def setup_inputs():
    n = np.random.standard_normal
    s = mx_kscale(K)[:, None]
    p_w = pack_weight(n((K, N)) / np.sqrt(K) / s, "e4m3")
    return {
        "xT": (n((K, T)) * s).astype(np.float32),
        "wgt": np.repeat(np.random.uniform(0.5, 2.0, (8, 3 * J)), 16, axis=0).astype(np.float32),
        "w_words": p_w[0],
        "w_scales": p_w[1],
        "b": (0.3 * n(N)).astype(np.float32),
        "offs": striped8(np.stack([np.concatenate([np.random.permutation(T)[:J] for _ in range(3)]) for _ in range(8)])),
    }


def reference(xT, wgt, w_words, w_scales, b, offs):
    idx = unstriped8(offs)
    rows = np.arange(K)
    xg = f64(wgt)[rows // 4 % 128] * f64(xT)[rows[:, None], idx[rows % 512 // 64]]
    xT_ = mxq(xg, 0, "e4m3").reshape(K, 3, J)
    w_ = unpack_weight(w_words, w_scales, "e4m3")
    a0 = w_.T @ xT_[:, 0]
    a1 = w_.T @ xT_[:, 1]
    a2 = w_.T @ xT_[:, 2]
    return gelu(np.maximum(np.maximum(a0, a1), a2) + f64(b)[:, None])

@@ -1,0 +1,143 @@
+from contextlib import ExitStack
+
+import concourse.mybir as mybir
+
+K, N, T, J = 512, 512, 2048, 512
+PICKS = 3
+P = 128
+PACK = 4
+FLOPS = 2 * K * N * J * PICKS
+
+F32 = mybir.dt.float32
+BF16 = mybir.dt.bfloat16
+I32 = mybir.dt.int32
+U32 = mybir.dt.uint32
+U16 = mybir.dt.uint16
+U8 = mybir.dt.uint8
+FP8X4 = mybir.dt.float8_e4m3fn_x4
+MULT = mybir.AluOpType.mult
+MAX = mybir.AluOpType.max
+GELU = mybir.ActivationFunctionType.Gelu_apprx_tanh
+
+M_TILES = N // P
+LAST = 256
+
+
+def tile_list_max_gelu_kernel(tc, xT, wgt, w_words, w_scales, b, offs, out):
+    nc = tc.nc
+    with ExitStack() as ctx:
+        keep = ctx.enter_context(tc.tile_pool(name="keep", bufs=1))
+        psum = ctx.enter_context(tc.psum_pool(name="psum", bufs=1))
+
+        offsets = keep.tile([P, PICKS * J // 16], U16, name="offsets")
+        nc.sync.dma_start(offsets[:], offs)
+
+        warm = keep.tile([P, 8], F32, name="warm")
+        warm_out = keep.tile([P, 8], F32, name="warm_out")
+        nc.vector.memset(warm[:], 0.0)
+        nc.scalar.activation(warm_out[:], warm[:], GELU)
+
+        w_planes = keep.tile([P, N], U8, name="w_planes", align_bytes=64)
+        nc.vector.memset(w_planes[:].bitcast(I32), 0)
+
+        rows = xT.rearrange("(p i) t -> p i t", i=PACK)
+        planes = [keep.tile([P, T], F32, name=f"plane{i}") for i in range(PACK)]
+        w_codes = keep.tile([P, N], U32, name="w_codes", align_bytes=64)
+        bias = keep.tile([P, M_TILES], F32, name="bias")
+        H = LAST
+        area_a = keep.tile([P, PACK * J], F32, name="area_a")
+        area_b = keep.tile([P, H + PACK * J], F32, name="area_b")
+        wgt0 = area_a[:, H : H + J]
+        wgt1 = area_a[:, H + J : H + 2 * J]
+        wgt2 = keep.tile([P, J], F32, name="wgt2")
+        picked0 = area_b[:, H:].rearrange("p (i s) -> p i s", i=PACK)
+        picked1 = keep.tile([P, PACK, J], F32, name="picked1")
+        picked2 = [area[:, 0 : PACK * J].rearrange("p (i s) -> p i s", i=PACK)[:, :, 0:H] for area in (area_a, area_b)]
+
+        nc.sync.dma_start(planes[0][:], rows[:, 0, :])
+        nc.sync.dma_start(wgt0, wgt[:, 0:J])
+        nc.sync.dma_start(wgt1, wgt[:, J : 2 * J])
+        nc.sync.dma_start(wgt2[:], wgt[:, 2 * J : 3 * J])
+        for i in range(1, PACK):
+            nc.sync.dma_start(planes[i][:], rows[:, i, :])
+        nc.sync.dma_start(w_codes[:].bitcast(I32), w_words[0].rearrange("p n i -> p (n i)").bitcast(I32))
+        for q in range(4):
+            nc.sync.dma_start(w_planes[32 * q : 32 * q + 4, :].bitcast(I32), w_scales[0, 4 * q : 4 * q + 4, :].bitcast(I32))
+        with nc.allow_non_contiguous_dma(reason="one bias value a partition"):
+            nc.sync.dma_start(bias[:], b.rearrange("(m p) -> p m", p=P))
+
+        def gather(dst, i, weights, first, count):
+            nc.vector.tensor_tensor(dst, planes[i][:].indirect(offsets[:, first // 16 : (first + count) // 16]), weights, MULT)
+
+        def weave(src, width, name):
+            grouped = keep.tile([P, width, PACK], BF16, name="grouped_" + name, align_bytes=64)
+            nc.scalar.copy(
+                grouped[:].rearrange("p (c e) i -> p c i e", e=4),
+                src.rearrange("p i (c e) -> p c i e", e=4),
+            )
+            return grouped
+
+        def quantise(grouped, width, name):
+            codes = keep.tile([P, width], U32, name="codes_" + name, align_bytes=64)
+            scales = keep.tile([P, width], U8, name="scales_" + name, align_bytes=64)
+            nc.vector.quantize_mx(codes[:].bitcast(FP8X4), scales[:], grouped[:].rearrange("p s i -> p (s i)"))
+            return codes, scales
+
+        def project(acc, m, operand):
+            codes, scales = operand
+            cols = slice(m * P, (m + 1) * P)
+            nc.tensor.matmul_mx(acc, lhsT=w_codes[:, cols].bitcast(FP8X4), lhsT_scale=w_planes[:, cols],
+                                rhs=codes[:].bitcast(FP8X4), rhs_scale=scales[:], start=True, stop=True)
+
+        def gather2(h, i):
+            gather(picked2[h][:, i, :], i, wgt2[:, h * H : (h + 1) * H], 2 * J + h * H, H)
+
+        for i in range(PACK):
+            gather(picked0[:, i, :], i, wgt0, 0, J)
+            if i == PACK - 1:
+                grouped0 = weave(picked0, J, "c0")
+            gather(picked1[:, i, :], i, wgt1, J, J)
+            if i == 0:
+                gather2(0, 0)
+                gather2(1, 0)
+        grouped1 = weave(picked1[:], J, "c1")
+        for i in range(1, PACK):
+            gather2(0, i)
+        op0 = quantise(grouped0, J, "c0")
+        acc0 = [psum.tile([P, J], F32, name=f"acc0_{m}", tag=f"bank{m}") for m in range(M_TILES)]
+        for m in range(M_TILES):
+            project(acc0[m][:], m, op0)
+        for i in range(1, PACK):
+            gather2(1, i)
+        op1 = quantise(grouped1, J, "c1")
+        acc1 = [psum.tile([P, J], F32, name=f"acc1_{m}", tag=f"bank{4 + m}") for m in range(M_TILES)]
+        for m in range(M_TILES):
+            project(acc1[m][:], m, op1)
+
+        first = [keep.tile([P, J], F32, name=f"first{m}") for m in range(M_TILES)]
+        best = [keep.tile([P, 2, J], F32, name=f"best{mb}") for mb in range(2)]
+        op2 = []
+        for h in range(2):
+            for m in (2 * h, 2 * h + 1):
+                nc.scalar.copy(first[m][:], acc0[m][:])
+            grouped2 = weave(picked2[h], H, f"c2_{h}")
+            for m in (2 * h, 2 * h + 1):
+                nc.vector.tensor_tensor(best[h][:, m % 2, :], acc1[m][:], first[m][:], MAX)
+            op2.append(quantise(grouped2, H, f"c2_{h}"))
+
+        out_tiles = out.rearrange("(m p) j -> p m j", p=P)
+        for h in range(2):
+            cols = slice(h * H, (h + 1) * H)
+            for mb in range(2):
+                acc2 = psum.tile([P, 2, H], F32, name=f"acc2_{h}_{mb}", tag=f"bank{2 * h + mb}")
+                for u in range(2):
+                    project(acc2[:, u, :], 2 * mb + u, op2[h])
+                parts = [(0, 1), (1, 2)] if (h, mb) == (1, 1) else [(0, 2)]
+                for lo, hi in parts:
+                    pooled = keep.tile([P, hi - lo, H], F32, name=f"pooled_{h}_{mb}_{lo}")
+                    nc.vector.tensor_tensor(pooled[:], acc2[:, lo:hi, :], best[mb][:, lo:hi, cols], MAX)
+                    result = keep.tile([P, hi - lo, H], F32, name=f"result_{h}_{mb}_{lo}")
+                    for u in range(lo, hi):
+                        m = 2 * mb + u
+                        nc.scalar.activation(result[:, u - lo, :], pooled[:, u - lo, :], GELU, bias=bias[:, m : m + 1])
+                    nc.sync.dma_start(out_tiles[:, 2 * mb + lo : 2 * mb + hi, cols], result[:])

@@ -45,99 +45,126 @@ def tile_list_max_gelu_kernel(tc, xT, wgt, w_words, w_scales, b, offs, out):
         w_codes = keep.tile([P, N], U32, name="w_codes", align_bytes=64)
         bias = keep.tile([P, M_TILES], F32, name="bias")
         H = LAST
-        area_a = keep.tile([P, PACK * J], F32, name="area_a")
-        area_b = keep.tile([P, H + PACK * J], F32, name="area_b")
-        wgt0 = area_a[:, H : H + J]
-        wgt1 = area_a[:, H + J : H + 2 * J]
-        wgt2 = keep.tile([P, J], F32, name="wgt2")
-        picked0 = area_b[:, H:].rearrange("p (i s) -> p i s", i=PACK)
-        picked1 = keep.tile([P, PACK, J], F32, name="picked1")
-        picked2 = [area[:, 0 : PACK * J].rearrange("p (i s) -> p i s", i=PACK)[:, :, 0:H] for area in (area_a, area_b)]
+        picked_a = [keep.tile([P, PACK, H], F32, name=f"picked_a{c}") for c in range(PICKS)]
+        area0 = keep.tile([P, PACK * H], F32, name="area0", tag="late0")
+        area1 = keep.tile([P, PACK * 2 * H], F32, name="area1", tag="late1")
+        area2 = keep.tile([P, PACK * H], F32, name="area2", tag="late2")
+        wgt0b = keep.tile([P, H], F32, name="wgt0b")
+        wgt2b = keep.tile([P, H], F32, name="wgt2b")
+        picked = {(c, 0): picked_a[c][:] for c in range(PICKS)}
+        picked[0, 1] = area0[:].rearrange("p (i s) -> p i s", i=PACK)
+        picked[1, 1] = area1[:].rearrange("p (i s) -> p i s", i=PACK)[:, :, 0:H]
+        picked[2, 1] = area2[:].rearrange("p (i s) -> p i s", i=PACK)
+        weights = {
+            (0, 0): area0[:, 2 * H : 3 * H],
+            (0, 1): wgt0b[:],
+            (1, 0): area1[:, 2 * H : 3 * H],
+            (1, 1): area1[:, 3 * H : 4 * H],
+            (2, 0): area1[:, 4 * H : 5 * H],
+            (2, 1): wgt2b[:],
+        }
 
         nc.sync.dma_start(planes[0][:], rows[:, 0, :])
-        nc.sync.dma_start(wgt0, wgt[:, 0:J])
-        nc.sync.dma_start(wgt1, wgt[:, J : 2 * J])
-        nc.sync.dma_start(wgt2[:], wgt[:, 2 * J : 3 * J])
+        nc.sync.dma_start(weights[0, 0], wgt[:, 0:H])
+        nc.sync.dma_start(weights[0, 1], wgt[:, H : 2 * H])
+        nc.sync.dma_start(area1[:, 2 * H : 5 * H], wgt[:, 2 * H : 5 * H])
         for i in range(1, PACK):
             nc.sync.dma_start(planes[i][:], rows[:, i, :])
+        nc.sync.dma_start(weights[2, 1], wgt[:, 5 * H : 6 * H])
         nc.sync.dma_start(w_codes[:].bitcast(I32), w_words[0].rearrange("p n i -> p (n i)").bitcast(I32))
         for q in range(4):
             nc.sync.dma_start(w_planes[32 * q : 32 * q + 4, :].bitcast(I32), w_scales[0, 4 * q : 4 * q + 4, :].bitcast(I32))
         with nc.allow_non_contiguous_dma(reason="one bias value a partition"):
             nc.sync.dma_start(bias[:], b.rearrange("(m p) -> p m", p=P))
 
-        def gather(dst, i, weights, first, count):
-            nc.vector.tensor_tensor(dst, planes[i][:].indirect(offsets[:, first // 16 : (first + count) // 16]), weights, MULT)
+        def gather(c, h, i):
+            first = (c * J + h * H) // 16
+            nc.vector.tensor_tensor(picked[c, h][:, i, :], planes[i][:].indirect(offsets[:, first : first + H // 16]), weights[c, h], MULT)
 
-        def weave(src, width, name):
-            grouped = keep.tile([P, width, PACK], BF16, name="grouped_" + name, align_bytes=64)
+        def weave(c, h):
+            grouped = keep.tile([P, H, PACK], BF16, name=f"grouped{c}{h}", align_bytes=64)
             nc.scalar.copy(
-                grouped[:].rearrange("p (c e) i -> p c i e", e=4),
-                src.rearrange("p i (c e) -> p c i e", e=4),
+                grouped[:].rearrange("p (s e) i -> p s i e", e=4),
+                picked[c, h].rearrange("p i (s e) -> p s i e", e=4),
             )
             return grouped
 
-        def quantise(grouped, width, name):
-            codes = keep.tile([P, width], U32, name="codes_" + name, align_bytes=64)
-            scales = keep.tile([P, width], U8, name="scales_" + name, align_bytes=64)
+        def project(c, h, grouped, banks):
+            codes = keep.tile([P, H], U32, name=f"codes{c}{h}", align_bytes=64)
+            scales = keep.tile([P, H], U8, name=f"scales{c}{h}", align_bytes=64)
             nc.vector.quantize_mx(codes[:].bitcast(FP8X4), scales[:], grouped[:].rearrange("p s i -> p (s i)"))
-            return codes, scales
+            sums = []
+            for k, bank in enumerate(banks):
+                acc = psum.tile([P, 2, H], F32, name=f"acc{c}{h}{k}", tag=f"bank{bank}")
+                for u in range(2):
+                    cols = slice((2 * k + u) * P, (2 * k + u + 1) * P)
+                    nc.tensor.matmul_mx(acc[:, u, :], lhsT=w_codes[:, cols].bitcast(FP8X4), lhsT_scale=w_planes[:, cols],
+                                        rhs=codes[:].bitcast(FP8X4), rhs_scale=scales[:], start=True, stop=True)
+                sums.append(acc)
+            return sums
 
-        def project(acc, m, operand):
-            codes, scales = operand
-            cols = slice(m * P, (m + 1) * P)
-            nc.tensor.matmul_mx(acc, lhsT=w_codes[:, cols].bitcast(FP8X4), lhsT_scale=w_planes[:, cols],
-                                rhs=codes[:].bitcast(FP8X4), rhs_scale=scales[:], start=True, stop=True)
-
-        def gather2(h, i):
-            gather(picked2[h][:, i, :], i, wgt2[:, h * H : (h + 1) * H], 2 * J + h * H, H)
-
-        for i in range(PACK):
-            gather(picked0[:, i, :], i, wgt0, 0, J)
-            if i == PACK - 1:
-                grouped0 = weave(picked0, J, "c0")
-            gather(picked1[:, i, :], i, wgt1, J, J)
-            if i == 0:
-                gather2(0, 0)
-                gather2(1, 0)
-        grouped1 = weave(picked1[:], J, "c1")
-        for i in range(1, PACK):
-            gather2(0, i)
-        op0 = quantise(grouped0, J, "c0")
-        acc0 = [psum.tile([P, J], F32, name=f"acc0_{m}", tag=f"bank{m}") for m in range(M_TILES)]
-        for m in range(M_TILES):
-            project(acc0[m][:], m, op0)
-        for i in range(1, PACK):
-            gather2(1, i)
-        op1 = quantise(grouped1, J, "c1")
-        acc1 = [psum.tile([P, J], F32, name=f"acc1_{m}", tag=f"bank{4 + m}") for m in range(M_TILES)]
-        for m in range(M_TILES):
-            project(acc1[m][:], m, op1)
-
-        first = [keep.tile([P, J], F32, name=f"first{m}") for m in range(M_TILES)]
-        best = [keep.tile([P, 2, J], F32, name=f"best{mb}") for mb in range(2)]
-        op2 = []
-        for h in range(2):
-            for m in (2 * h, 2 * h + 1):
-                nc.scalar.copy(first[m][:], acc0[m][:])
-            grouped2 = weave(picked2[h], H, f"c2_{h}")
-            for m in (2 * h, 2 * h + 1):
-                nc.vector.tensor_tensor(best[h][:, m % 2, :], acc1[m][:], first[m][:], MAX)
-            op2.append(quantise(grouped2, H, f"c2_{h}"))
+        def leave(sums, h):
+            held = []
+            for k in range(2):
+                first = keep.tile([P, 2, H], F32, name=f"first{h}{k}")
+                nc.scalar.copy(first[:], sums[k][:])
+                held.append(first)
+            return held
 
         out_tiles = out.rearrange("(m p) j -> p m j", p=P)
-        for h in range(2):
-            cols = slice(h * H, (h + 1) * H)
-            for mb in range(2):
-                acc2 = psum.tile([P, 2, H], F32, name=f"acc2_{h}_{mb}", tag=f"bank{2 * h + mb}")
-                for u in range(2):
-                    project(acc2[:, u, :], 2 * mb + u, op2[h])
-                parts = [(0, 1), (1, 2)] if (h, mb) == (1, 1) else [(0, 2)]
-                for lo, hi in parts:
-                    pooled = keep.tile([P, hi - lo, H], F32, name=f"pooled_{h}_{mb}_{lo}")
-                    nc.vector.tensor_tensor(pooled[:], acc2[:, lo:hi, :], best[mb][:, lo:hi, cols], MAX)
-                    result = keep.tile([P, hi - lo, H], F32, name=f"result_{h}_{mb}_{lo}")
-                    for u in range(lo, hi):
-                        m = 2 * mb + u
-                        nc.scalar.activation(result[:, u - lo, :], pooled[:, u - lo, :], GELU, bias=bias[:, m : m + 1])
-                    nc.sync.dma_start(out_tiles[:, 2 * mb + lo : 2 * mb + hi, cols], result[:])
+
+        def finish(pooled, h, m0, count):
+            result = keep.tile([P, count, H], F32, name=f"result{h}{m0}")
+            for u in range(count):
+                nc.scalar.activation(result[:, u, :], pooled[:, u, :], GELU, bias=bias[:, m0 + u : m0 + u + 1])
+            nc.sync.dma_start(out_tiles[:, m0 : m0 + count, h * H : (h + 1) * H], result[:])
+
+        for c, h in ((0, 0), (0, 1), (1, 0), (2, 0), (1, 1)):
+            gather(c, h, 0)
+        for c, h in ((0, 0), (1, 0), (2, 0), (0, 1)):
+            gather(c, h, 1)
+        grouped = {}
+        for i in (2, 3):
+            for c in range(PICKS):
+                gather(c, 0, i)
+                if i == PACK - 1:
+                    grouped[c, 0] = weave(c, 0)
+        sums = {}
+        sums[0, 0] = project(0, 0, grouped[0, 0], (0, 1))
+        sums[1, 0] = project(1, 0, grouped[1, 0], (2, 3))
+        sums[2, 0] = project(2, 0, grouped[2, 0], (4, 5))
+        held_a = leave(sums[0, 0], 0)
+        for c in range(PICKS):
+            for i in range(2 - c, PACK):
+                gather(c, 1, i)
+            grouped[c, 1] = weave(c, 1)
+        sums[0, 1] = project(0, 1, grouped[0, 1], (6, 7))
+        best_a = keep.tile([P, M_TILES, H], F32, name="best_a", tag="late0")
+        for k in range(2):
+            nc.vector.tensor_tensor(best_a[:, 2 * k : 2 * k + 2, :], sums[1, 0][k][:], held_a[k][:], MAX)
+        sums[1, 1] = project(1, 1, grouped[1, 1], (0, 1))
+        pooled_a = [keep.tile([P, 2, H], F32, name=f"pooled_a{k}", tag=f"late{k + 1}") for k in range(2)]
+        nc.vector.tensor_tensor(pooled_a[0][:], sums[2, 0][0][:], best_a[:, 0:2, :], MAX)
+        sums[2, 1] = project(2, 1, grouped[2, 1], (2, 3))
+        nc.vector.tensor_tensor(pooled_a[1][:], sums[2, 0][1][:], best_a[:, 2:4, :], MAX)
+        held_b = leave(sums[0, 1], 1)
+        for k in range(2):
+            finish(pooled_a[k], 0, 2 * k, 2)
+        best_b = [keep.tile([P, count, H], F32, name=f"best_b{m0}") for m0, count in ((0, 2), (2, 1), (3, 1))]
+
+        def pool_first(n, m0, count):
+            u = m0 % 2
+            nc.vector.tensor_tensor(best_b[n][:], sums[1, 1][m0 // 2][:, u : u + count, :], held_b[m0 // 2][:, u : u + count, :], MAX)
+
+        def pool_last(n, m0, count):
+            u = m0 % 2
+            pooled = keep.tile([P, count, H], F32, name=f"pooled_b{m0}")
+            nc.vector.tensor_tensor(pooled[:], sums[2, 1][m0 // 2][:, u : u + count, :], best_b[n][:], MAX)
+            finish(pooled, 1, m0, count)
+
+        pool_first(0, 0, 2)
+        pool_first(1, 2, 1)
+        pool_last(0, 0, 2)
+        pool_first(2, 3, 1)
+        pool_last(1, 2, 1)
+        pool_last(2, 3, 1)

@@ -29,7 +29,11 @@ def tile_list_max_gelu_kernel(tc, xT, wgt, w_words, w_scales, b, offs, out):
         keep = ctx.enter_context(tc.tile_pool(name="keep", bufs=1))
         psum = ctx.enter_context(tc.psum_pool(name="psum", bufs=1))
 
+        H = LAST
+        rows = xT.rearrange("(p i) t -> p i t", i=PACK)
+        planes = [keep.tile([P, T], F32, name=f"plane{i}") for i in range(PACK)]
         offsets = keep.tile([P, PICKS * J // 16], U16, name="offsets")
+        nc.sync.dma_start(planes[0][:], rows[:, 0, :])
         nc.sync.dma_start(offsets[:], offs)
 
         warm = keep.tile([P, 8], F32, name="warm")
@@ -40,34 +44,34 @@ def tile_list_max_gelu_kernel(tc, xT, wgt, w_words, w_scales, b, offs, out):
         w_planes = keep.tile([P, N], U8, name="w_planes", align_bytes=64)
         nc.vector.memset(w_planes[:].bitcast(I32), 0)
 
-        rows = xT.rearrange("(p i) t -> p i t", i=PACK)
-        planes = [keep.tile([P, T], F32, name=f"plane{i}") for i in range(PACK)]
         w_codes = keep.tile([P, N], U32, name="w_codes", align_bytes=64)
         bias = keep.tile([P, M_TILES], F32, name="bias")
-        H = LAST
-        picked_a = [keep.tile([P, PACK, H], F32, name=f"picked_a{c}") for c in range(PICKS)]
         area0 = keep.tile([P, PACK * H], F32, name="area0", tag="late0")
-        area1 = keep.tile([P, PACK * 2 * H], F32, name="area1", tag="late1")
-        area2 = keep.tile([P, PACK * H], F32, name="area2", tag="late2")
+        area1 = keep.tile([P, (PACK + 1) * H], F32, name="area1", tag="late1")
+        early1 = keep.tile([P, PACK, H], F32, name="early1", tag="late2")
+        early2 = keep.tile([P, PACK, H], F32, name="early2")
         wgt0b = keep.tile([P, H], F32, name="wgt0b")
+        wgt_mid = keep.tile([P, 3 * H], F32, name="wgt_mid")
         wgt2b = keep.tile([P, H], F32, name="wgt2b")
-        picked = {(c, 0): picked_a[c][:] for c in range(PICKS)}
-        picked[0, 1] = area0[:].rearrange("p (i s) -> p i s", i=PACK)
-        picked[1, 1] = area1[:].rearrange("p (i s) -> p i s", i=PACK)[:, :, 0:H]
-        picked[2, 1] = area2[:].rearrange("p (i s) -> p i s", i=PACK)
+        picked = {
+            (0, 0): area1[:, H:].rearrange("p (i s) -> p i s", i=PACK),
+            (1, 0): early1[:],
+            (2, 0): early2[:],
+            (0, 1): area0[:].rearrange("p (i s) -> p i s", i=PACK),
+            (1, 1): area1[:, 0 : PACK * H].rearrange("p (i s) -> p i s", i=PACK),
+        }
         weights = {
             (0, 0): area0[:, 2 * H : 3 * H],
             (0, 1): wgt0b[:],
-            (1, 0): area1[:, 2 * H : 3 * H],
-            (1, 1): area1[:, 3 * H : 4 * H],
-            (2, 0): area1[:, 4 * H : 5 * H],
+            (1, 0): wgt_mid[:, 0:H],
+            (1, 1): wgt_mid[:, H : 2 * H],
+            (2, 0): wgt_mid[:, 2 * H : 3 * H],
             (2, 1): wgt2b[:],
         }
 
-        nc.sync.dma_start(planes[0][:], rows[:, 0, :])
         nc.sync.dma_start(weights[0, 0], wgt[:, 0:H])
         nc.sync.dma_start(weights[0, 1], wgt[:, H : 2 * H])
-        nc.sync.dma_start(area1[:, 2 * H : 5 * H], wgt[:, 2 * H : 5 * H])
+        nc.sync.dma_start(wgt_mid[:], wgt[:, 2 * H : 5 * H])
         for i in range(1, PACK):
             nc.sync.dma_start(planes[i][:], rows[:, i, :])
         nc.sync.dma_start(weights[2, 1], wgt[:, 5 * H : 6 * H])
@@ -134,6 +138,8 @@ def tile_list_max_gelu_kernel(tc, xT, wgt, w_words, w_scales, b, offs, out):
         sums[1, 0] = project(1, 0, grouped[1, 0], (2, 3))
         sums[2, 0] = project(2, 0, grouped[2, 0], (4, 5))
         held_a = leave(sums[0, 0], 0)
+        late2 = keep.tile([P, PACK, H], F32, name="late2", tag="late2")
+        picked[2, 1] = late2[:]
         for c in range(PICKS):
             for i in range(2 - c, PACK):
                 gather(c, 1, i)
@@ -150,21 +156,25 @@ def tile_list_max_gelu_kernel(tc, xT, wgt, w_words, w_scales, b, offs, out):
         held_b = leave(sums[0, 1], 1)
         for k in range(2):
             finish(pooled_a[k], 0, 2 * k, 2)
-        best_b = [keep.tile([P, count, H], F32, name=f"best_b{m0}") for m0, count in ((0, 2), (2, 1), (3, 1))]
+        best_b = [keep.tile([P, 2, H], F32, name=f"best_b{k}") for k in range(2)]
 
-        def pool_first(n, m0, count):
-            u = m0 % 2
-            nc.vector.tensor_tensor(best_b[n][:], sums[1, 1][m0 // 2][:, u : u + count, :], held_b[m0 // 2][:, u : u + count, :], MAX)
+        def pool_first(m0, count):
+            k, u = divmod(m0, 2)
+            nc.vector.tensor_tensor(best_b[k][:, u : u + count, :], sums[1, 1][k][:, u : u + count, :], held_b[k][:, u : u + count, :], MAX)
 
-        def pool_last(n, m0, count):
-            u = m0 % 2
-            pooled = keep.tile([P, count, H], F32, name=f"pooled_b{m0}")
-            nc.vector.tensor_tensor(pooled[:], sums[2, 1][m0 // 2][:, u : u + count, :], best_b[n][:], MAX)
-            finish(pooled, 1, m0, count)
+        def pool_last(m, lo, hi):
+            k, u = divmod(m, 2)
+            pooled = keep.tile([P, hi - lo], F32, name=f"pooled_b{m}_{lo}")
+            nc.vector.tensor_tensor(pooled[:], sums[2, 1][k][:, u, lo:hi], best_b[k][:, u, lo:hi], MAX)
+            result = keep.tile([P, hi - lo], F32, name=f"result_b{m}_{lo}")
+            nc.scalar.activation(result[:], pooled[:], GELU, bias=bias[:, m : m + 1])
+            nc.sync.dma_start(out_tiles[:, m, H + lo : H + hi], result[:])
 
-        pool_first(0, 0, 2)
-        pool_first(1, 2, 1)
-        pool_last(0, 0, 2)
-        pool_first(2, 3, 1)
-        pool_last(1, 2, 1)
-        pool_last(2, 3, 1)
+        pool_first(0, 2)
+        pool_first(2, 1)
+        pool_last(0, 0, H)
+        pool_last(1, 0, H)
+        pool_first(3, 1)
+        pool_last(2, 0, H)
+        pool_last(3, 0, H // 2)
+        pool_last(3, H // 2, H)

from contextlib import ExitStack

import concourse.mybir as mybir

K, N, T, J = 512, 512, 2048, 512
PICKS = 3
P = 128
PACK = 4
FLOPS = 2 * K * N * J * PICKS

F32 = mybir.dt.float32
BF16 = mybir.dt.bfloat16
I32 = mybir.dt.int32
U32 = mybir.dt.uint32
U16 = mybir.dt.uint16
U8 = mybir.dt.uint8
FP8X4 = mybir.dt.float8_e4m3fn_x4
MULT = mybir.AluOpType.mult
MAX = mybir.AluOpType.max
GELU = mybir.ActivationFunctionType.Gelu_apprx_tanh

M_TILES = N // P
LAST = 256


def tile_list_max_gelu_kernel(tc, xT, wgt, w_words, w_scales, b, offs, out):
    nc = tc.nc
    with ExitStack() as ctx:
        keep = ctx.enter_context(tc.tile_pool(name="keep", bufs=1))
        psum = ctx.enter_context(tc.psum_pool(name="psum", bufs=1))

        H = LAST
        rows = xT.rearrange("(p i) t -> p i t", i=PACK)
        planes = [keep.tile([P, T], F32, name=f"plane{i}") for i in range(PACK)]
        offsets = keep.tile([P, PICKS * J // 16], U16, name="offsets")
        nc.sync.dma_start(planes[0][:], rows[:, 0, :])
        nc.sync.dma_start(offsets[:], offs)

        warm = keep.tile([P, 8], F32, name="warm")
        warm_out = keep.tile([P, 8], F32, name="warm_out")
        nc.vector.memset(warm[:], 0.0)
        nc.scalar.activation(warm_out[:], warm[:], GELU)

        w_planes = keep.tile([P, N], U8, name="w_planes", align_bytes=64)
        nc.vector.memset(w_planes[:].bitcast(I32), 0)

        w_codes = keep.tile([P, N], U32, name="w_codes", align_bytes=64)
        bias = keep.tile([P, M_TILES], F32, name="bias")
        area0 = keep.tile([P, PACK * H], F32, name="area0", tag="late0")
        area1 = keep.tile([P, (PACK + 1) * H], F32, name="area1", tag="late1")
        early1 = keep.tile([P, PACK, H], F32, name="early1", tag="late2")
        early2 = keep.tile([P, PACK, H], F32, name="early2")
        wgt0b = keep.tile([P, H], F32, name="wgt0b")
        wgt_mid = keep.tile([P, 3 * H], F32, name="wgt_mid")
        wgt2b = keep.tile([P, H], F32, name="wgt2b")
        picked = {
            (0, 0): area1[:, H:].rearrange("p (i s) -> p i s", i=PACK),
            (1, 0): early1[:],
            (2, 0): early2[:],
            (0, 1): area0[:].rearrange("p (i s) -> p i s", i=PACK),
            (1, 1): area1[:, 0 : PACK * H].rearrange("p (i s) -> p i s", i=PACK),
        }
        weights = {
            (0, 0): area0[:, 2 * H : 3 * H],
            (0, 1): wgt0b[:],
            (1, 0): wgt_mid[:, 0:H],
            (1, 1): wgt_mid[:, H : 2 * H],
            (2, 0): wgt_mid[:, 2 * H : 3 * H],
            (2, 1): wgt2b[:],
        }

        nc.sync.dma_start(weights[0, 0], wgt[:, 0:H])
        nc.sync.dma_start(weights[0, 1], wgt[:, H : 2 * H])
        nc.sync.dma_start(wgt_mid[:], wgt[:, 2 * H : 5 * H])
        for i in range(1, PACK):
            nc.sync.dma_start(planes[i][:], rows[:, i, :])
        nc.sync.dma_start(weights[2, 1], wgt[:, 5 * H : 6 * H])
        nc.sync.dma_start(w_codes[:].bitcast(I32), w_words[0].rearrange("p n i -> p (n i)").bitcast(I32))
        for q in range(4):
            nc.sync.dma_start(w_planes[32 * q : 32 * q + 4, :].bitcast(I32), w_scales[0, 4 * q : 4 * q + 4, :].bitcast(I32))
        with nc.allow_non_contiguous_dma(reason="one bias value a partition"):
            nc.sync.dma_start(bias[:], b.rearrange("(m p) -> p m", p=P))

        def gather(c, h, i):
            first = (c * J + h * H) // 16
            nc.vector.tensor_tensor(picked[c, h][:, i, :], planes[i][:].indirect(offsets[:, first : first + H // 16]), weights[c, h], MULT)

        def weave(c, h):
            grouped = keep.tile([P, H, PACK], BF16, name=f"grouped{c}{h}", align_bytes=64)
            nc.scalar.copy(
                grouped[:].rearrange("p (s e) i -> p s i e", e=4),
                picked[c, h].rearrange("p i (s e) -> p s i e", e=4),
            )
            return grouped

        def project(c, h, grouped, banks):
            codes = keep.tile([P, H], U32, name=f"codes{c}{h}", align_bytes=64)
            scales = keep.tile([P, H], U8, name=f"scales{c}{h}", align_bytes=64)
            nc.vector.quantize_mx(codes[:].bitcast(FP8X4), scales[:], grouped[:].rearrange("p s i -> p (s i)"))
            sums = []
            for k, bank in enumerate(banks):
                acc = psum.tile([P, 2, H], F32, name=f"acc{c}{h}{k}", tag=f"bank{bank}")
                for u in range(2):
                    cols = slice((2 * k + u) * P, (2 * k + u + 1) * P)
                    nc.tensor.matmul_mx(acc[:, u, :], lhsT=w_codes[:, cols].bitcast(FP8X4), lhsT_scale=w_planes[:, cols],
                                        rhs=codes[:].bitcast(FP8X4), rhs_scale=scales[:], start=True, stop=True)
                sums.append(acc)
            return sums

        def leave(sums, h):
            held = []
            for k in range(2):
                first = keep.tile([P, 2, H], F32, name=f"first{h}{k}")
                nc.scalar.copy(first[:], sums[k][:])
                held.append(first)
            return held

        out_tiles = out.rearrange("(m p) j -> p m j", p=P)

        def finish(pooled, h, m0, count):
            result = keep.tile([P, count, H], F32, name=f"result{h}{m0}")
            for u in range(count):
                nc.scalar.activation(result[:, u, :], pooled[:, u, :], GELU, bias=bias[:, m0 + u : m0 + u + 1])
            nc.sync.dma_start(out_tiles[:, m0 : m0 + count, h * H : (h + 1) * H], result[:])

        for c, h in ((0, 0), (0, 1), (1, 0), (2, 0), (1, 1)):
            gather(c, h, 0)
        for c, h in ((0, 0), (1, 0), (2, 0), (0, 1)):
            gather(c, h, 1)
        grouped = {}
        for i in (2, 3):
            for c in range(PICKS):
                gather(c, 0, i)
                if i == PACK - 1:
                    grouped[c, 0] = weave(c, 0)
        sums = {}
        sums[0, 0] = project(0, 0, grouped[0, 0], (0, 1))
        sums[1, 0] = project(1, 0, grouped[1, 0], (2, 3))
        sums[2, 0] = project(2, 0, grouped[2, 0], (4, 5))
        held_a = leave(sums[0, 0], 0)
        late2 = keep.tile([P, PACK, H], F32, name="late2", tag="late2")
        picked[2, 1] = late2[:]
        for c in range(PICKS):
            for i in range(2 - c, PACK):
                gather(c, 1, i)
            grouped[c, 1] = weave(c, 1)
        sums[0, 1] = project(0, 1, grouped[0, 1], (6, 7))
        best_a = keep.tile([P, M_TILES, H], F32, name="best_a", tag="late0")
        for k in range(2):
            nc.vector.tensor_tensor(best_a[:, 2 * k : 2 * k + 2, :], sums[1, 0][k][:], held_a[k][:], MAX)
        sums[1, 1] = project(1, 1, grouped[1, 1], (0, 1))
        pooled_a = [keep.tile([P, 2, H], F32, name=f"pooled_a{k}", tag=f"late{k + 1}") for k in range(2)]
        nc.vector.tensor_tensor(pooled_a[0][:], sums[2, 0][0][:], best_a[:, 0:2, :], MAX)
        sums[2, 1] = project(2, 1, grouped[2, 1], (2, 3))
        nc.vector.tensor_tensor(pooled_a[1][:], sums[2, 0][1][:], best_a[:, 2:4, :], MAX)
        held_b = leave(sums[0, 1], 1)
        for k in range(2):
            finish(pooled_a[k], 0, 2 * k, 2)
        best_b = [keep.tile([P, 2, H], F32, name=f"best_b{k}") for k in range(2)]

        def pool_first(m0, count):
            k, u = divmod(m0, 2)
            nc.vector.tensor_tensor(best_b[k][:, u : u + count, :], sums[1, 1][k][:, u : u + count, :], held_b[k][:, u : u + count, :], MAX)

        def pool_last(m, lo, hi):
            k, u = divmod(m, 2)
            pooled = keep.tile([P, hi - lo], F32, name=f"pooled_b{m}_{lo}")
            nc.vector.tensor_tensor(pooled[:], sums[2, 1][k][:, u, lo:hi], best_b[k][:, u, lo:hi], MAX)
            result = keep.tile([P, hi - lo], F32, name=f"result_b{m}_{lo}")
            nc.scalar.activation(result[:], pooled[:], GELU, bias=bias[:, m : m + 1])
            nc.sync.dma_start(out_tiles[:, m, H + lo : H + hi], result[:])

        pool_first(0, 2)
        pool_first(2, 1)
        pool_last(0, 0, H)
        pool_last(1, 0, H)
        pool_first(3, 1)
        pool_last(2, 0, H)
        pool_last(3, 0, H // 2)
        pool_last(3, H // 2, H)
